import numpy as np, ml_dtypes
CORES = [6,15,38,47]
N = 4
BF = ml_dtypes.bfloat16
def f(rng, *shape):
    return (rng.standard_normal(shape, dtype=np.float32) * np.exp2(rng.integers(-2, 3, shape[:-1] + (1,)))).astype(BF)
def wide(rng, *shape):
    v = f(rng, *shape).astype(np.float32); k = shape[:-2] + (1, shape[-1])
    return (v * np.exp2(rng.integers(-6, 7, k)) * (rng.random(k) > 0.0625)).astype(BF)
W, L, T, C, TH, SH = 4096, 256, 4, 4, 11, 12
def at(tab, a):
    return np.take_along_axis(tab, a.reshape(tab.shape[:-1] + (-1,)), -1).reshape(a.shape)
def tax(rng, key):
    term = np.argsort(key, axis=-1); gap = W - 1 - np.argsort(term, axis=-1)
    def up(lo, hi):
        v = np.where(rng.random((N, 8, W)) < 0.75, rng.random((1, 8, W)), rng.random((N, 8, W)))
        return np.take_along_axis(np.broadcast_to(term, (N, 8, W)), W - 1 - (gap * (lo + (hi - lo) * v)).astype(np.int64), 2)
    return term, gap, up(0.3, 0.7), up(0.05, 0.4)
def heights(rng, gap):
    h = (1.5 * (SH - np.log2(gap + 1.0))).astype(np.float32)[None, :, None, :]
    e = (h + rng.standard_normal((N, 8, 16, W), dtype=np.float32)) * np.exp2(rng.integers(-2, 3, (N, 8, 16, 1))).astype(np.float32)
    return e.reshape(N, 128, W).astype(BF)
def low(rng, term, n, top):
    return np.take_along_axis(np.broadcast_to(term, (N, 8, W)), rng.integers(0, top, (N, 8, n)), 2)
def lanes(rng, term, p0, p1):
    s = low(rng, term, 16 * L, W // 2).reshape(N, 8, 16, L)
    z = np.where(rng.random((N, 8, 16 * T * L)) < 0.1, low(rng, term, 16 * T * L, W), low(rng, term, 16 * T * L, W // 2)).reshape(N, 8, 16, T, L)
    kind = rng.integers(0, 8, (N, 8, 1, L))
    d = np.where(kind < 4, rng.integers(2, C + 1, s.shape), rng.integers(1, C + 1, s.shape)); d = np.where((kind < 3) & (rng.random(s.shape) < 0.1), 1, d)
    a = s
    for i in range(C):
        nx = at(p0, a)
        if i == 0: nx = np.where(rng.random(s.shape) < 0.4, at(p1, a), nx)
        a = np.where(d > i, nx, a)
    g = np.where(kind == 7, low(rng, term, 16 * L, W).reshape(s.shape), a)
    return s, g, z, (rng.random((N, 8, T, L)) < 0.4).astype(np.int64)
def pack(e, pa, s, g, z, sg):
    i4 = lambda v, *sh: np.ascontiguousarray(np.reshape(v, (N,) + sh)).astype(np.int32)
    return {"ev": np.reshape(e, (N, 128, W)).astype(BF), "par": i4(pa, 8, W), "s0": i4(s, 128, L), "g0": i4(g, 128, L), "z": i4(z, 128, T * L), "sg": i4(sg, 8, T * L)}
def setup_inputs(rng):
    term, gap, p0, p1 = tax(rng, rng.random((8, W)))
    return pack(heights(rng, gap), p0 + W * p1, *lanes(rng, term, p0, p1))
def setup_inputs_corners(rng):
    term, gap, p0, p1 = tax(rng, rng.random((8, W))); own = np.arange(W); c = rng.integers(0, 7, (1, 8, W))
    p0 = np.where(c == 0, own, np.where((c == 1) | (c == 4), W - 1, np.where((c == 2) | (c == 3), 0, p0)))
    p1 = np.where((c == 0) | (c == 3), own, np.where(c == 1, W - 1, np.where((c == 2) | (c == 4), 0, p1)))
    b = np.where(np.arange(N)[:, None, None] == 0, own, W - 1); p0 = np.where(c == 6, b, p0); p1 = np.where(c == 6, b, p1)
    for p in (p0, p1): p[:, ::2, W - 1] = W - 1; p[:, 1::2, W - 1] = 0
    e = heights(rng, gap).astype(np.float32); e[:, :, 0] = -256.0; e[:, :, W - 1] = 256.0
    s, g, z, sg = lanes(rng, term, p0, p1); one = (N, 8, 1, L)
    n = rng.choice(np.array([0, 0, 1, 4, 5, 16]), one); k = np.argsort(rng.random(s.shape), axis=2)
    g = np.where(rng.random(one) < 0.8, np.where(k < n, 0, W - 1), g)
    same = rng.random(one) < 0.2; s = np.where(same, s[:, :, :1], s); z = np.where(same[:, :, :, None], z[:, :, :1], z)
    g = np.where(rng.random(one) < 0.08, s, g); m = rng.integers(0, 8, (N, 8, 1, T, L))
    z = np.where(m == 0, s[:, :, :, None], np.where((m == 1) & (rng.random(z.shape) < 0.5), W - 1, np.where((m == 2) & (rng.random(z.shape) < 0.3), 0, z)))
    sg[0, :, 0] = 0; sg[1, :, 0] = 1; sg[2, :, 0] = 1; g[0] = W - 1
    for h in range(8):
        o = np.nonzero(c[0, h, 1:W - 1] == 0)[0] + 1; v = np.nonzero(c[0, h, 1:W - 1] == 6)[0] + 1
        s[0, h] = np.where(rng.random((1, L)) < 0.4, rng.choice(o, (16, L)), rng.choice(v, (16, L)))
        a, u = rng.permutation(v)[:2]; w = e[:, 16 * h:16 * h + 16]
        w[1:, :, a] = w[1:, :, u]; w[1, rng.permutation(16)[TH:], a] = -256.0
        j = np.append(rng.permutation(L - 1)[:L // 8], L - 1); i = rng.integers(0, 16, j.size)
        s[0, h, :, j] = rng.choice(o, (j.size, 16)); s[0, h, i, j] = a; z[0, h, i, 0, j] = u
    s[2, 7, :, L - 1] = rng.choice(o, 16); g[2, 7, :, L - 1] = W - 1; sg[2, 7, 0, L - 1] = 0
    for h in range(8):
        o = np.nonzero(c[0, h, 1:W - 1] == 0)[0] + 1; j = L if h < 7 else 1
        s[N - 1, h, :, :j] = rng.choice(o, (16, j)); g[N - 1, h, :, :j] = W - 1; sg[N - 1, h, 0] = 1; sg[N - 1, h, 0, :j] = 0
    return pack(e, p0 + W * p1, s, g, z, sg)
def setup_inputs_ends(rng):
    term, gap, p0, p1 = tax(rng, rng.random((8, W))); e = heights(rng, gap).astype(np.float32).reshape(N, 8, 16, W)
    cnt = rng.choice(np.array([0, 16, 8, 7, TH, TH - 1]), (N, 8, 1)); cnt[:, 0] = 16; cnt[:, 7] = 0
    v = np.where(np.argsort(rng.random((N, 8, 16)), axis=2) < cnt, 32.0, -32.0); v[:, 3] = 0.0
    e[..., 0] = v; e[..., W - 1] = -v
    pa = np.where(rng.random((N, 8, W)) < 0.85, (W * W - 1) * rng.integers(0, 2, (N, 8, W)), p0 + W * p1)
    kind = rng.integers(0, 5, (N, 8)); kind[:, 0] = 0; kind[:, 7] = 0; kind[N - 1] = 2
    pa[:, :, 0] = np.array([W * W - 1, 0, W * W - 1, 0, W - 1])[kind]; pa[:, :, W - 1] = np.array([0, W * W - 1, W * W - 1, 0, W * (W - 1)])[kind]
    def ends(*t):
        sh = (N, 8, 16) + t + (L,); one = (N, 8, 1) + t + (L,)
        x = np.where(rng.random(one) < 0.5, (W - 1) * rng.integers(0, 2, one), (W - 1) * rng.integers(0, 2, sh))
        return np.where((rng.random(one) < 0.25) & (rng.random(sh) < 0.5), rng.integers(0, W, sh), x)
    s = ends(); g = ends(); z = ends(T); sg = rng.integers(0, 2, (N, 8, T, L))
    x = (W - 1) * rng.integers(0, 2, (8, 16, L)); s[N - 1] = x; g[N - 1] = x; z[N - 1, :, :, 0] = x; sg[N - 1, :, 0] = 0; sg[1, :, 0] = 1
    s[:N - 1, 7, :, L - 3:] = 0; g[:N - 1, 7, :, L - 2:] = W - 1; g[:N - 1, 7, :, L - 3] = 0
    z[:N - 1, 7, :, 0, L - 3:] = W - 1; z[:N - 1, 7, :15, 0, L - 1] = 0; sg[:N - 1, 7, 0, L - 3:] = np.array([1, 0, 0])
    return pack(e, pa, s, g, z, sg)
def setup_inputs_spread(rng):
    c = rng.integers(-6, 7, (8, W)); term, gap, p0, p1 = tax(rng, c + rng.random((8, W)))
    w = np.abs(wide(rng, N, 128, W).astype(np.float32)).reshape(N, 8, 16, W) * np.exp2(2.0 * c).astype(np.float32)[None, :, None, :]
    w = np.where(rng.random((N, 8, 16, 1)) < 0.06, -w, w)
    return pack(w, p0 + W * p1, *lanes(rng, term, p0, p1))
def setup_inputs_ties(rng):
    term, gap, p0, p1 = tax(rng, rng.random((8, W))); q = W // 8; top = gap < q
    x = rng.integers(0, 4, (N, 8, 16, W)); x = np.where(top[None, :, None, :] & (rng.random(x.shape) < 0.75), 3, x)
    x[:, 5] = x[:, 5] // 2; x[:, 2] = 1
    u = np.take_along_axis(term[:, W - q:], rng.integers(0, q, (8, W)), 1)[None]
    p0 = np.where(rng.random((N, 8, W)) < 0.9, u, p0); p1 = np.where(rng.random((1, 8, W)) < 0.6, p0, p1)
    s, g, z, sg = lanes(rng, term, p0, p1); g = np.where(rng.random((N, 8, 1, L)) < 0.7, at(p0, s), g)
    return pack(x.astype(np.float32), p0 + W * p1, s, g, z, sg)
def check_inputs(d):
    bad = []
    for k, hi in (("par", W * W - 1), ("s0", W - 1), ("g0", W - 1), ("z", W - 1), ("sg", 1)):
        if np.min(d[k]) < 0 or np.max(d[k]) > hi: bad.append("range of " + k)
    e = d["ev"].astype(np.float32)
    if not np.all(np.isfinite(e)): bad.append("ev is not finite")
    if np.any((e != 0) & (np.abs(e) < np.float32(2.0 ** -126))): bad.append("ev holds subnormal numbers")
    return bad
def wits(tab, a):
    return np.take_along_axis(tab, a.reshape(8, 1, -1), 2).reshape(8, 16, 16, L)
def reference(ev, par, s0, g0, z, sg):
    e = ev.astype(np.float32).reshape(N, 8, 16, W); pa = par.astype(np.int64); p0 = pa & (W - 1); p1 = pa >> SH
    zs = z.astype(np.int64).reshape(N, 8, 16, T, L); plus = sg.reshape(N, 8, T, L) == 1
    S = s0.astype(np.int64).reshape(N, 8, 16, L); G = g0.astype(np.int64).reshape(N, 8, 16, L)
    ride = np.zeros((N, 8, L), bool); rz = np.zeros((N, 8, 16, L), np.int64)
    for t in range(T):
        for r in range(N):
            q = (r + t) % N; th = TH + (int(np.sum(ride[r])) & 1)
            x = np.where(ride[r][:, None], rz[r], zs[q, :, :, t]); pos = (plus[q, :, t] & ~ride[r])[:, None]
            ex = wits(e[q], x); g = G[r]; a = S[r]
            miss = np.sum(np.sum(wits(e[q], g) >= ex, axis=1) < th, axis=1)[:, None]
            for i in range(C):
                cov = np.sum(wits(e[q], a) >= ex, axis=1)
                nx = np.where(cov >= 8, at(p0[q], a), at(p1[q], a))
                stop = np.where(pos, cov >= th, nx == g)
                a = np.where(stop, a, nx)
            full = ~pos & (miss == 0); can = full & stop & (cov < th)
            win = np.argmin(np.where(can, cov, 99), axis=1)
            hit = can & (np.arange(16)[None, :, None] == win[:, None])
            S[r] = np.where(pos, a, S[r]); G[r] = np.where((pos & (miss > 4)) | hit, a, g)
            ride[r] = full[:, 0] & ~np.any(can, axis=1); rz[r] = x
    return {"ys": S.reshape(N, 128, L).astype(np.float32), "yg": G.reshape(N, 128, L).astype(np.float32)}

@@ -1,0 +1,430 @@
+import math
+from concourse.mybir import AluOpType as ALU, ActivationFunctionType as AF
+
+NB = 4
+LB = 256 // NB
+NV = 4
+W = 4096
+ND = [16384, 12288, 8192, 4096]
+LN2 = math.log(2.0)
+LAT = 4.0
+CY, C_GATH, C_PE = 0.00083, 1.56, 0.00042
+PAR = [4.45, 3.66, 1.19, 0.0, 0.15, 0.0, 0.0, 1]
+
+SCRATCH = {}
+for _n, _k, _t in (("EV", 5 * W, 0), ("PW", 4 * W, 0), ("EX", W, 0), ("GE", W, 0), ("GEG", W, 0), ("PG", W, 0),
+                   ("SI", 256, 2), ("GI", 256, 2), ("ZI", 1024, 2), ("ZN", 1024, 1), ("PARI", 256, 2), ("PCI", 1024, 2),
+                   ("PCB", 1024, 0), ("LST", 512, 3), ("LA", 256, 3), ("XL", 256, 3), ("XF", 256, 1), ("PB", 256, 1),
+                   ("G2", 512, 1), ("PM", 256, 0), ("MM", 256, 0), ("UU", 256, 0), ("FF", 512, 0), ("T1", 256, 1),
+                   ("AA", 256, 1), ("AM", 256, 2), ("AI", 256, 2), ("IF", 128, 1), ("MS", 256, 0), ("NF", 256, 0),
+                   ("UPD", 256, 0), ("C2", 256, 0), ("MV", 256, 0), ("WW", 256, 0), ("WIN", 256, 0), ("SGN", 256, 0),
+                   ("SGM", 512, 2), ("CNT", 32, 1), ("PARC", 4, 2), ("PARB", 4, 2), ("PARF", 4, 1), ("TB", 16, 1),
+                   ("LAND", 9 * 256, 2), ("PKT", 9 * 256, 2), ("LANDF", 512, 1), ("PKF", 512, 1), ("ONE", 144, 0),
+                   ("XS", 512, 1), ("T8", 256, 0), ("CC", 256, 0), ("B1", 144, 0), ("B2", 144, 0), ("WC", 144, 0),
+                   ("W0", 144, 0), ("W1", 144, 0), ("I1", 128, 0), ("BOH", 128, 0), ("BON", 128, 0), ("ON32", 128, 1),
+                   ("KI", 1, 2), ("KK", 1, 2), ("KC", 8, 1), ("DG", 128 * 6, 0)):
+    SCRATCH[_n] = ("sbuf", [128, _k], ("bfloat16", "float32", "int32", "uint16")[_t])
+SCRATCH["SGI"] = ("sbuf", [8, 1024], "int32")
+SCRATCH["NSG"] = ("sbuf", [8, 1024], "bfloat16")
+SCRATCH["E1"] = ("sbuf", [8, 128], "bfloat16")
+SCRATCH["EN"] = ("sbuf", [8, 512], "bfloat16")
+for _n in range(8):
+    SCRATCH["pb%d" % _n] = ("psum", [128, 512], "float32")
+DIAG = [16.0, 32.0, 20480.0, 40960.0, -32768.0, 32768.0]
+SEMAPHORES = (["qV", "qS", "qP", "qG", "sent"] + ["d%d" % i for i in range(32)]
+              + ["arr%d_%d" % (t, b) for t in range(1, 5) for b in range(NB)])
+QS = {"V": "qV", "S": "qS", "P": "qP", "G": "qG"}
+
+
+def build(g, core, T, topo):
+    rank = T.rank_of(core)
+    nxt, prv = T.cores[(rank + 1) % 4], T.cores[(rank + 3) % 4]
+    n_out, n_arr = len(topo.engines(core, nxt)), len(topo.engines(prv, core))
+    rid, pid = topo.addr(nxt)[:2]
+    msk = topo.mask(core, nxt)
+    ops = []
+    ndma = [0]
+    cur = [0]
+    v, s, te = g.vector, g.scalar, g.tensor
+
+    def op(q, dur, fn, rd=(), wr=(), lat=0.0, sem=None, inc=1, name=""):
+        ops.append({"q": q, "dur": dur, "lat": lat, "fn": fn, "rd": list(rd), "wr": list(wr), "sem": sem, "inc": inc,
+                    "name": name, "i": len(ops), "b": cur[0]})
+
+    def dma(q, out, in_, rd, wr, us):
+        ndma[0] += 1
+        e = g.sync if q == "Y" else s
+        op(q, 0.07, lambda: e.dma_start(out, in_), rd, wr, lat=us, sem="d%d" % (ndma[0] - 1), inc=16, name="dma")
+
+    def vec(n, fn, rd, wr, name=""):
+        op("V", max(64, n) * CY + 0.01, fn, rd, wr, name=name)
+
+    def tt(out, a, b, o, rd, wr, n=LB, name=""):
+        vec(n, lambda: v.tensor_tensor(out, a, b, o), rd, wr, name)
+
+    def ts(out, a, s1, s2, o0, o1, rd, wr, n=LB):
+        vec(n, (lambda: v.tensor_scalar(out, a, s1, s2, o0)) if o1 is None else (lambda: v.tensor_scalar(out, a, s1, s2, o0, o1)), rd, wr)
+
+    def cp(out, a, rd, wr, n=LB):
+        vec(n, lambda: v.tensor_copy(out, a), rd, wr)
+
+    def fill(out, x, wr, n):
+        vec(n, lambda: v.memset(out, x), [], wr)
+
+    def act(out, a, f, rd, wr, n=LB, **kw):
+        op("S", max(64, n) * CY + 0.03, lambda: s.activation(out, a, f, **kw), rd, wr)
+
+    def mm(calls, cols, rd, wr):
+        def fn():
+            for c in calls:
+                x = te.matmul(*c)
+            return x
+        op("P", cols * C_PE + 0.02, fn, rd, wr)
+
+    def dg(c):
+        i = DIAG.index(c)
+        return T.DG[:, 128 * i:128 * i + 128]
+
+    def dk(*c):
+        return ["DG%g" % x for x in c]
+
+    def col(n, t, w=256):
+        return T[n][:, w * t:w * t + w]
+
+    dma("Y", T.PARI[:], T.par[:], [], ["PARI"], 2.0)
+    dma("S", col("ZI", 0), T.z[:, 0:256], [], ["ZI0"], 2.0)
+    dma("Y", T.EV[:, 0:W], T.ev[:], [], ["EV0"], 6.0)
+    dma("S", T.SI[:], T.s0[:], [], ["SI"], 2.5)
+    dma("S", T.SGI[:], T.sg[:], [], ["SGI"], 2.5)
+    dma("S", T.GI[:], T.g0[:], [], ["GI"], 3.0)
+    fill(T.ONE[:], 1.0, ["ONE"], 72)
+    fill(T.PW[:, 0:W], 0.0, ["PW0m"], 2048)
+    fill(T.SGN[:], -1.0, ["SGN"], 64)
+    op("G", 0.15, lambda: g.iota(T.KI[:], [[0, 1]], 0, 1), [], ["KI"])
+
+    def sel(out, a, pat, cop, base, cm, rd, wr):
+        op("G", 0.4, lambda: g.affine_select(out, a, pat, cop, 0.0, base, cm), [rd], [wr])
+    sel(T.B1[:], T.ONE[:], [[-16, 9], [0, 16]], ALU.is_ge, 0, 1, "ONE", "B1")
+    sel(T.B2[:], T.B1[:], [[16, 9], [0, 16]], ALU.is_ge, 15, -1, "B1", "B2")
+    sel(T.WC[:], T.B2[:], [[0, 9], [1, 16]], ALU.is_equal, -15, 0, "B2", "WC")
+    sel(T.I1[:], T.ONE[:, 0:128], [[-1, 128]], ALU.is_equal, 0, 1, "ONE", "I1")
+    sel(T.E1[:], T.ONE[0:8, 0:128], [[1, 8], [0, 16]], ALU.is_equal, 0, -1, "ONE", "E1")
+    for i in range(4):
+        ts(col("PCI", i), T.PARI[:], 6 * i, 63, ALU.logical_shift_right, ALU.bitwise_and, ["PARI"], ["PCI%d" % i], 256)
+    for i in range(4):
+        cp(col("PCB", i), col("PCI", i), ["PCI%d" % i], ["PCB%d" % i], 256)
+        dma("Y", T.PW[i::16, 0:W], col("PCB", i), ["PCB%d" % i, "PW0m"], ["PW0p%d" % i], 2.0)
+    PW0 = ["PW0m"] + ["PW0p%d" % i for i in range(4)]
+    kc = [T.KC[:, i:i + 1] for i in range(7)]
+    ts(T.KK[:], T.KI[:], 15, None, ALU.bitwise_and, None, ["KI"], ["KK"], 1)
+    for i in range(4):
+        ts(kc[i], T.KK[:], float(i), (1.0, 64.0)[i % 2], ALU.is_equal, ALU.mult, ["KK"], ["KC%d" % i], 1)
+    for i in range(2):
+        tt(kc[4 + i], kc[2 * i], kc[2 * i + 1], ALU.add, ["KC%d" % (2 * i), "KC%d" % (2 * i + 1)], ["KW%d" % i], 1)
+        ts(T["W%d" % i][:], T.WC[:], kc[4 + i], None, ALU.mult, None, ["WC", "KW%d" % i], ["W%d" % i], 72)
+    ts(kc[6], T.KK[:], -LN2, -160.0 * LN2, ALU.mult, ALU.add, ["KK"], ["KE"], 1)
+    for c, x in enumerate((-26.0, 6.0, -10.5, 0.0)):
+        fill(T.TB[:, c:c + 1], x, ["TB0_%d" % c], 1)
+    TB0 = ["TB0_%d" % c for c in range(4)]
+    for c in DIAG:
+        ts(dg(c), T.I1[:], c, None, ALU.mult, None, ["I1"], dk(c), 64)
+    ts(T.BOH[:], T.B2[:, 0:128], 0.5, None, ALU.mult, None, ["B2"], ["BOH"], 64)
+    ts(T.BON[:], T.B2[:, 0:128], -0.5, None, ALU.mult, None, ["B2"], ["BON"], 64)
+    for t in range(NV):
+        if t:
+            dma("Y", col("ZI", t), T.z[:, 256 * t:256 * t + 256], [], ["ZI%d" % t], 2.0)
+        ts(col("NSG", t), col("SGI", t), -1.0, 1.0, ALU.mult, ALU.add, ["SGI"], ["NSG%d" % t], 256)
+        ts(col("EN", t, 128), T.E1[:], float(ND[t]), None, ALU.mult, None, ["E1"], ["EN%d" % t], 64)
+        bk, pt = "ps%d" % t, T["pb%d" % t][:, 0:256]
+        mm([(pt, col("EN", t, 128), col("NSG", t), True, True)], 256, ["EN%d" % t, "NSG%d" % t], [bk])
+        tt(col("ZN", t), col("ZI", t), pt, ALU.add, ["ZI%d" % t, bk], ["ZN%d" % t], 256)
+    fill(T.ON32[:], 1.0 / 32, ["ON32"], 128)
+    cp(T.IF[:], T.I1[:], ["I1"], ["IF"], 128)
+    for r in range(1, 4):
+        dma("Y", col("EV", r, W), T.ev[:], [], ["EV%d" % r], 6.0)
+        dma("Y", col("PW", r, W), T.PW[:, 0:W], PW0, ["PW%d" % r], 6.0)
+    dma("Y", col("EV", 4, W), T.ev[:], [], ["EV4"], 6.0)
+
+    def EVk(n):
+        return ["EV%d" % r for r in range(n)]
+
+    def PWk(n):
+        return PW0 + ["PW%d" % r for r in range(1, n)]
+
+    def visit(t):
+        last = t == NV - 1
+        st = {}
+
+        def env(b):
+            cur[0] = b
+            return (lambda n: col(n, b, LB), lambda n: col(n, b, 2 * LB), lambda n: col(n, b, 16 * LB), lambda n: "%s_%d" % (n, b),
+                    T["pb%d" % b], "ps%d" % b, T["pb%d" % (4 + b)], "ps%d" % (4 + b))
+
+        def strided(buf, b, k):
+            return T[buf][:, 16 * LB * b + k:16 * LB * (b + 1):16]
+
+        def begin(b):
+            f1, f2, f16, K, X, kX, Cb, kC = env(b)
+            if t == 0:
+                S_, G_, SG_, kS, kG = f1("SI"), f1("GI"), None, "SI", "GI"
+                xf, kx, n = f1("ZN"), "ZN0", 1
+                cp(f1("XL"), f1("ZI"), ["ZI0"], [K("XL")])
+                cp(col("LST", 2 * b, LB), S_, [kS], [K("LS")])
+                cp(col("LST", 2 * b + 1, LB), G_, [kG], [K("LG")])
+            else:
+                o = ((t - 1) * NB + b) * 3 * LB
+                S_, G_, R_, SG_ = (T.LAND[:, o + x * LB:o + y * LB] for x, y in ((0, 1), (1, 2), (2, 3), (0, 2)))
+                kS = kG = "LAND%d_%d" % (t, b)
+                xf, kx, n = f1("XF"), K("XF"), 5
+                tt(xf, col("ZN", NB * t + b, LB), R_, ALU.max, ["ZN%d" % t, kS], [kx], 2 * LB)
+                cp(f1("XL"), xf, [kx], [K("XL")])
+                cp(f2("LST"), SG_, [kS], [K("LS"), K("LG")], 2 * LB)
+            act(f16("EX"), T.EV[:, 0:n * W].indirect(f1("XL")), AF.Copy, EVk(n) + [K("XL")], [K("EX")], 16 * LB * C_GATH)
+            act(f1("PM"), xf, AF.Sign, [kx], [K("PM")], bias=4095.5, scale=-1.0)
+            if t:
+                act(f1("MV"), xf, AF.Sign, [kx], [K("MV"), "CNT%d_%d" % (t, b)], bias=-(ND[t - 1] - 0.5), accum_out=T.CNT[:, 8 * t + b:8 * t + b + 1])
+            act(f1("T8"), f1("PM"), AF.Copy, [K("PM")], [K("T8")], scale=16.0, bias=8.0)
+            act(f1("PB"), f1("PM"), AF.Relu, [K("PM")], [K("PB")], scale=8192.0)
+            ga, gb = col("G2", 2 * b, LB), col("G2", 2 * b + 1, LB)
+            tt(ga, G_, f1("PB"), ALU.max, [kG, K("PB")], [K("G2a")], 2 * LB)
+            act(gb, ga, AF.Copy, [K("G2a")], [K("G2b")])
+            st[b] = (S_, G_, SG_, kS, kG, xf, kx)
+
+        for b in range(NB):
+            begin(b)
+        TBk = TB0
+        if t:
+            pt, kb = T["pb%d" % (3 + NB)][:, 448:449], "ps%d" % (3 + NB)
+            c1, c2, c3 = (T[n][:, t:t + 1] for n in ("PARC", "PARB", "PARF"))
+            mm([(pt, T.ON32[:], T.CNT[:, 8 * t + j:8 * t + j + 1], j == 0, j == NB - 1) for j in range(NB)], 4 * 256,
+               ["ON32"] + ["CNT%d_%d" % (t, j) for j in range(NB)], [kb])
+            cp(c1, pt, [kb], ["PARC%d" % t], 1)
+            ts(c2, c1, 1, None, ALU.bitwise_and, None, ["PARC%d" % t], ["PARB%d" % t], 1)
+            cp(c3, c2, ["PARB%d" % t], ["PARF%d" % t], 1)
+            ts(T.TB[:, 4 * t:4 * t + 4], T.TB[:, 0:4], c3, None, ALU.subtract, None, TB0 + ["PARF%d" % t], ["TB%d" % t], 4)
+            TBk = ["TB%d" % t]
+        bU, bC, bM = (T.TB[:, 4 * t + j:4 * t + j + 1] for j in range(3))
+
+        def step(b, i):
+            f1, f2, f16, K, X, kX, Cb, kC = env(b)
+            S_, G_, SG_, kS, kG, xf, kx = st[b]
+            lst, kl = (col("LST", 2 * b, LB), K("LS")) if i == 0 else (f1("LA"), K("LA"))
+            a, ka = (S_, kS) if i == 0 else (f1("AI"), K("AI")) if t == 0 else (f1("AA"), K("AA"))
+            n = 1 if t == 0 else i + 1
+            C_, R_, X0, X1, X_ = Cb[:, 0:LB], X[:, 0:2 * LB], X[:, 2 * LB:3 * LB], X[:, 3 * LB:4 * LB], X[:, 2 * LB:4 * LB]
+            tt(f16("GE"), T.EV[:, 0:n * W].indirect(lst), f16("EX"), ALU.is_ge, EVk(n) + [kl, K("EX")], [K("GE")], 16 * LB * C_GATH)
+            act(f16("PG"), T.PW[:, 0:n * W].indirect(lst), AF.Copy, PWk(n) + [kl], [K("PG")], 16 * LB * C_GATH)
+            mm([(C_, dg(16.0), f1("PM"), True, False)] + [(C_, T.WC[:, 15 - k:143 - k], strided("GE", b, k), False, k == 15) for k in range(16)],
+               17 * LB, ["WC", K("GE"), K("PM")] + dk(16.0), [kC])
+            mm([(X[:, j * LB:j * LB + LB], w[:, 15 - k:143 - k], strided("PG", b, k), k == 0, k == 15) for j, w in enumerate((T.W0, T.W1)) for k in range(16)],
+               32 * LB, ["W0", "W1", K("PG")], [kX])
+            tt(f2("FF"), f2("G2"), R_, ALU.is_equal, [K("G2a"), K("G2b"), kX], [K("FF")], 2 * LB)
+            act(f2("XS"), R_, AF.Copy, [kX], [K("XS")], 2 * LB, bias=4096.0 * (i + 1))
+            tt(f1("MM"), f1("T8"), C_, ALU.is_le, [K("T8"), kC], [K("MM")])
+            act(f1("UU"), C_, AF.Relu, [kC] + TBk, [K("UU")], bias=bU)
+            P = -32768.0
+            mm([(X_, T.IF[:], f2("XS"), True, False), (X0, dg(P), T.ONE[:, 0:LB], False, False), (X_, dg(P), f2("FF"), False, False)],
+               11 * LB, dk(P) + ["IF", "ONE", K("XS"), K("FF")], [kX])
+            mm([(X0, dg(-P), f1("MM"), False, False), (X1, dg(P), f1("MM"), False, False)], 2 * LB, dk(P, -P) + [K("MM")], [kX])
+            mm([(X0, dg(P), f1("UU"), False, False), (X1, dg(P), f1("UU"), False, True)], 2 * LB, dk(P) + [K("UU")], [kX])
+            tt(f1("T1"), a, X0, ALU.max, [ka, kX], [K("T1")])
+            if t == 0 and i < 3:
+                tt(f1("AM"), f1("T1"), X1, ALU.max, [K("T1"), kX], [K("AM")])
+                ts(f1("AI"), f1("AM"), 4095, None, ALU.bitwise_and, None, [K("AM")], [K("AI")])
+                cp(f1("LA"), f1("AI"), [K("AI")], [K("LA")])
+                return
+            tt(f1("AA"), f1("T1"), X1, ALU.max, [K("T1"), kX], [K("AA")])
+            if i < 3:
+                cp(f1("LA"), f1("AA"), [K("AA")], [K("LA")])
+
+        def covg(b):
+            f1, f2, f16, K, X, kX, Cb, kC = env(b)
+            lst, cg, ms = col("LST", 2 * b + 1, LB), Cb[:, LB:2 * LB], Cb[:, 2 * LB:3 * LB]
+            tt(f16("GEG"), T.EV[:, 0:W].indirect(lst), f16("EX"), ALU.is_ge, EVk(1) + [K("LG"), K("EX")], [K("GEG")], 16 * LB * C_GATH, "covg")
+            mm([(cg, T.WC[:, 15 - k:143 - k], strided("GEG", b, k), k == 0, k == 15) for k in range(16)], 16 * LB, ["WC", K("GEG")], [kC])
+            act(f1("MS"), cg, AF.Sign, [kC] + TBk, [K("MS")], bias=bM)
+            mm([(ms, T.BON[:], f1("MS"), True, False), (ms, dg(32.0), f1("PM"), False, True)], 2 * LB, ["BON", K("MS"), K("PM")] + dk(32.0), [kC])
+            act(f1("NF"), ms, AF.Relu, [kC], [K("NF")], bias=40.0)
+            act(f1("UPD"), ms, AF.Relu, [kC], [K("UPD")], bias=-28.0)
+
+        def finish(b):
+            f1, f2, f16, K, X, kX, Cb, kC = env(b)
+            S_, G_, SG_, kS, kG, xf, kx = st[b]
+            C_, cw, sx, nr = Cb[:, 0:LB], Cb[:, 4 * LB:5 * LB], Cb[:, 3 * LB:4 * LB], Cb[:, 6 * LB:7 * LB]
+            p4, p5, p45 = X[:, 4 * LB:5 * LB], X[:, 5 * LB:6 * LB], X[:, 4 * LB:6 * LB]
+            act(f1("CC"), C_, AF.Copy, [kC], [K("CC")])
+            act(f1("C2"), C_, AF.Relu, [kC] + TBk, [K("C2")], bias=bC)
+            mm([(cw, T.I1[:], f1("CC"), True, False)] + [(cw, dg(32.0), f1(n), False, False) for n in ("NF", "C2")], 3 * LB,
+               dk(32.0) + ["I1", K("CC"), K("NF"), K("C2")], [kC])
+            act(f1("MV"), f1("AA"), AF.Relu, [K("AA")], [K("MV")], bias=-16383.0)
+            mm([(cw, dg(32.0), f1("MV"), False, True)], LB, dk(32.0) + [K("MV")], [kC])
+            act(f1("WW"), cw, AF.Exp, [kC, "KE"], [K("WW")], bias=kc[6], scale=-16.0 * LN2)
+            mm([(sx, T.BOH[:], f1("WW"), True, False), (sx, T.I1[:], f1("NF"), False, True)], 2 * LB, ["BOH", "I1", K("WW"), K("NF")], [kC])
+            tt(f1("WIN"), f1("WW"), sx, ALU.is_gt, [K("WW"), kC], [K("WIN")])
+            o = (t * NB + b) * 3 * LB
+            kp, ka, kb = "PKT%d_%d" % (t, b), K("SGMa"), K("SGMb")
+            if not last:
+                ts(nr, sx, 0.0, -65536.0, ALU.is_gt, ALU.mult, [kC], [kC])
+                tt(T.PKT[:, o + 2 * LB:o + 3 * LB], xf, nr, ALU.add, [kx, kC], [kp + "R"])
+            c1, c2 = 20480.0, 40960.0
+            mm([(p4, dg(c1), f1("PM"), True, False), (p4, T.IF[:], f1("AA"), False, True), (p5, dg(c1), f1("SGN"), True, False),
+                (p5, T.IF[:], f1("AA"), False, False), (p5, dg(c2), f1("UPD"), False, False)], 11 * LB,
+               dk(c1, c2) + ["IF", "SGN", K("PM"), K("UPD"), K("AA")], [kX])
+            mm([(p5, dg(c2), f1("WIN"), False, True)], LB, dk(c2) + [K("WIN")], [kX])
+            if t == 0:
+                tt(col("SGM", 2 * b, LB), S_, p4, ALU.max, [kS, kX], [ka])
+                tt(col("SGM", 2 * b + 1, LB), G_, p5, ALU.max, [kG, kX], [kb])
+            else:
+                tt(f2("SGM"), SG_, p45, ALU.max, [kS, kX], [ka, kb], 2 * LB)
+            out, src = (T.LANDF, T.PKF) if last else (T.LAND, T.PKT)
+            w, o = (2 * LB, 2 * LB * b) if last else (3 * LB, o)
+            if not last:
+                ts(T.PKT[:, o:o + 2 * LB], f2("SGM"), 4095, None, ALU.bitwise_and, None, [ka, kb], [kp + "S"], 2 * LB)
+            else:
+                ts(f2("SGM"), f2("SGM"), 4095, None, ALU.bitwise_and, None, [ka, kb], [ka, kb], 2 * LB)
+                cp(f2("PKF"), f2("SGM"), [ka, kb], [kp + "S"], 2 * LB)
+            sem, kl = "arr%d_%d" % (t + 1, b), "LAND%d_%d" % (t + 1, b)
+            op("G", 1.0, lambda: g.remote_dma(out[:, o:o + w], src[:, o:o + w], T.sem[sem], T.sem.sent, pid, rid, msk),
+               [kp + "S"] + ([] if last else [kp + "R"]), [kp + "sent"], sem="sent", inc=n_out, name="send")
+            op("R", 0.0, None, [kp + "sent"], [kl], lat=LAT - 1.0, sem=sem, inc=n_arr, name="arrive")
+            if last:
+                dma("Y", T.ys[:, LB * b:LB * b + LB], T.LANDF[:, o:o + LB], [kl], ["YS%d" % b], 2.0)
+                dma("S", T.yg[:, LB * b:LB * b + LB], T.LANDF[:, o + LB:o + 2 * LB], [kl], ["YG%d" % b], 2.0)
+
+        for b in range(NB):
+            step(b, 0)
+        for b in range(NB):
+            covg(b)
+        for i in range(1, 4):
+            for b in range(NB):
+                step(b, i)
+        for b in range(NB):
+            finish(b)
+
+    for t in range(NV):
+        visit(t)
+    return ops
+
+
+def link(ops):
+    lastw, readers, acc = {}, {}, {}
+    for o in ops:
+        dep = {}
+
+        def add(p, w):
+            if p is not o:
+                dep[p["i"]] = dep.get(p["i"], False) or w
+        for k in o["rd"] + o["wr"]:
+            if k[:2] == "ps":
+                for q, p in acc.get(k, {}).items():
+                    add(p, not (q == o["q"] and q in ("P", "S")))
+        for k in o["rd"]:
+            if k in lastw:
+                p = lastw[k]
+                add(p, not (k[:2] == "ps" and p["q"] == "P" and o["q"] == "P"))
+        for k in o["wr"]:
+            if k[:2] != "ps":
+                if k in lastw:
+                    add(lastw[k], True)
+                for p in readers.get(k, []):
+                    add(p, p["q"] != o["q"] or p["sem"] is not None)
+        for k in o["rd"]:
+            readers.setdefault(k, []).append(o)
+        for k in o["wr"]:
+            lastw[k] = o
+            readers[k] = []
+        for k in o["rd"] + o["wr"]:
+            if k[:2] == "ps":
+                acc.setdefault(k, {})[o["q"]] = o
+        o["dep"] = dep
+
+
+def schedule(ops, par=None):
+    par = par or PAR
+    wake = 0.08
+    n = len(ops)
+    succ = [[] for _ in range(n)]
+    for o in ops:
+        for p in o["dep"]:
+            succ[p].append(o["i"])
+    prio = [0.0] * n
+    x = int(par[7])
+    for o in reversed(ops):
+        m = 0.0
+        for j in succ[o["i"]]:
+            m = max(m, prio[j] + (wake if ops[j]["q"] != o["q"] else 0.0))
+        prio[o["i"]] = m + o["dur"] + o["lat"]
+    for o in ops:
+        x = (x * 1103515245 + 12345) % 2147483648
+        prio[o["i"]] += par[o["b"]] - (par[5] if o["name"] == "covg" else 0.0) + par[6] * (x / 2147483648.0 - 0.5)
+    left = [len(o["dep"]) for o in ops]
+    rdy = [0.0] * n
+    free = {}
+    avail = {i for i in range(n) if left[i] == 0}
+    while avail:
+        best = None
+        for i in avail:
+            o = ops[i]
+            t0 = rdy[i] if o["q"] == "R" else max(free.get(o["q"], 0.0), rdy[i])
+            key = (t0 + (par[4] if o["dur"] > 1.0 and o["q"] in "VS" else 0.0), -prio[i], i, t0)
+            if best is None or key < best:
+                best = key
+        i, t0 = best[2:]
+        avail.discard(i)
+        o = ops[i]
+        o["t0"] = t0
+        free[o["q"]] = t0 + o["dur"]
+        for j in succ[i]:
+            p = ops[j]
+            if p["q"] != o["q"]:
+                w = t0 + o["dur"] + o["lat"] + wake
+            else:
+                w = t0 + o["dur"] + (o["lat"] if p["dep"][i] else 0.0)
+            rdy[j] = max(rdy[j], w)
+            left[j] -= 1
+            if left[j] == 0:
+                avail.add(j)
+    return sorted(ops, key=lambda o: (o["t0"], o["i"])), max(o["t0"] + o["dur"] + o["lat"] for o in ops)
+
+
+def emit(g, T, ops):
+    queues = {"V": g.vector, "S": g.scalar, "P": g.tensor, "G": g, "Y": g.sync}
+    cnt = {}
+    for o in ops:
+        s = o["sem"] or QS[o["q"]]
+        cnt[s] = cnt.get(s, 0) + o["inc"]
+        o["tick"] = (s, cnt[s])
+    byi = {o["i"]: o for o in ops}
+    know = {q: {} for q in queues}
+    for o in ops:
+        if o["q"] == "R":
+            o["know"] = {o["tick"][0]: o["tick"][1]}
+            continue
+        base = dict(know[o["q"]])
+        e = queues[o["q"]]
+        for p in sorted((byi[p] for p, w in o["dep"].items() if w), key=lambda p: (-p["t0"], p["i"])):
+            s, c = p["tick"]
+            if base.get(s, 0) >= c:
+                continue
+            e.wait_ge(T.sem[s], c)
+            for s2, c2 in p["know"].items():
+                base[s2] = max(base.get(s2, 0), c2)
+            base[s] = max(base.get(s, 0), c)
+        know[o["q"]] = base
+        x = o["fn"]()
+        if o["name"] != "send":
+            x.then_inc(T.sem[o["tick"][0]], o["inc"])
+        o["know"] = dict(base)
+        o["know"][o["tick"][0]] = o["tick"][1]
+    for s, c in cnt.items():
+        g.wait_ge(T.sem[s], c)
+
+
+def rank_program(g, core, T, topo):
+    if T.rank_of(core) is None:
+        return
+    ops = build(g, core, T, topo)
+    link(ops)
+    ops, est = schedule(ops)
+    emit(g, T, ops)
+    return est

@@ -7,9 +7,12 @@ NV = 4
 W = 4096
 ND = [16384, 12288, 8192, 4096]
 LN2 = math.log(2.0)
-LAT = 4.0
-CY, C_GATH, C_PE = 0.00083, 1.56, 0.00042
-PAR = [4.45, 3.66, 1.19, 0.0, 0.15, 0.0, 0.0, 1]
+LAT = 7.0
+CY, C_GATH, C_PE, WAKE = 0.00083, 1.2, 0.00045, 0.25
+PAR = [[6.75, 3.44, 1.87, 0.0], 0.3,
+       [[0.0, 0.0, 1.1, 0.0, 0.0, 0.0, 0.0], [0.0, 0.0, 0.6, 0.0, 0.0, 0.0, 0.0], [0.0, 0.5, -0.8, 0.0, 0.0, 0.0, 0.0], [0.3, 0.0, 0.2, 0.0, 0.0, 0.0, 1.1]]]
+TRIES = 400
+ORDER = {}
 
 SCRATCH = {}
 for _n, _k, _t in (("EV", 5 * W, 0), ("PW", 4 * W, 0), ("EX", W, 0), ("GE", W, 0), ("GEG", W, 0), ("PG", W, 0),
@@ -44,23 +47,23 @@ def build(g, core, T, topo):
     msk = topo.mask(core, nxt)
     ops = []
     ndma = [0]
-    cur = [0]
+    cur = [0, 0]
     v, s, te = g.vector, g.scalar, g.tensor
 
     def op(q, dur, fn, rd=(), wr=(), lat=0.0, sem=None, inc=1, name=""):
         ops.append({"q": q, "dur": dur, "lat": lat, "fn": fn, "rd": list(rd), "wr": list(wr), "sem": sem, "inc": inc,
-                    "name": name, "i": len(ops), "b": cur[0]})
+                    "name": name, "i": len(ops), "b": cur[0], "st": cur[1]})
 
     def dma(q, out, in_, rd, wr, us):
         ndma[0] += 1
         e = g.sync if q == "Y" else s
         op(q, 0.07, lambda: e.dma_start(out, in_), rd, wr, lat=us, sem="d%d" % (ndma[0] - 1), inc=16, name="dma")
 
-    def vec(n, fn, rd, wr, name=""):
-        op("V", max(64, n) * CY + 0.01, fn, rd, wr, name=name)
+    def vec(n, fn, rd, wr):
+        op("V", max(64, n) * CY + 0.01, fn, rd, wr)
 
-    def tt(out, a, b, o, rd, wr, n=LB, name=""):
-        vec(n, lambda: v.tensor_tensor(out, a, b, o), rd, wr, name)
+    def tt(out, a, b, o, rd, wr, n=LB):
+        vec(n, lambda: v.tensor_tensor(out, a, b, o), rd, wr)
 
     def ts(out, a, s1, s2, o0, o1, rd, wr, n=LB):
         vec(n, (lambda: v.tensor_scalar(out, a, s1, s2, o0)) if o1 is None else (lambda: v.tensor_scalar(out, a, s1, s2, o0, o1)), rd, wr)
@@ -91,14 +94,14 @@ def build(g, core, T, topo):
     def col(n, t, w=256):
         return T[n][:, w * t:w * t + w]
 
-    dma("Y", T.PARI[:], T.par[:], [], ["PARI"], 2.0)
-    dma("S", col("ZI", 0), T.z[:, 0:256], [], ["ZI0"], 2.0)
     dma("Y", T.EV[:, 0:W], T.ev[:], [], ["EV0"], 6.0)
+    dma("S", T.PARI[:], T.par[:], [], ["PARI"], 2.0)
+    dma("S", col("ZI", 0), T.z[:, 0:256], [], ["ZI0"], 2.0)
     dma("S", T.SI[:], T.s0[:], [], ["SI"], 2.5)
     dma("S", T.SGI[:], T.sg[:], [], ["SGI"], 2.5)
     dma("S", T.GI[:], T.g0[:], [], ["GI"], 3.0)
     fill(T.ONE[:], 1.0, ["ONE"], 72)
-    fill(T.PW[:, 0:W], 0.0, ["PW0m"], 2048)
+    fill(T.PW[:, 0:W], 1.0, ["PW0m"], 2048)
     fill(T.SGN[:], -1.0, ["SGN"], 64)
     op("G", 0.15, lambda: g.iota(T.KI[:], [[0, 1]], 0, 1), [], ["KI"])
 
@@ -115,17 +118,20 @@ def build(g, core, T, topo):
         cp(col("PCB", i), col("PCI", i), ["PCI%d" % i], ["PCB%d" % i], 256)
         dma("Y", T.PW[i::16, 0:W], col("PCB", i), ["PCB%d" % i, "PW0m"], ["PW0p%d" % i], 2.0)
     PW0 = ["PW0m"] + ["PW0p%d" % i for i in range(4)]
-    kc = [T.KC[:, i:i + 1] for i in range(7)]
+    kc = [T.KC[:, i:i + 1] for i in range(8)]
     ts(T.KK[:], T.KI[:], 15, None, ALU.bitwise_and, None, ["KI"], ["KK"], 1)
     for i in range(4):
         ts(kc[i], T.KK[:], float(i), (1.0, 64.0)[i % 2], ALU.is_equal, ALU.mult, ["KK"], ["KC%d" % i], 1)
+    ts(kc[7], T.KK[:], 4.0, 32768.0, ALU.is_equal, ALU.mult, ["KK"], ["KC7"], 1)
     for i in range(2):
         tt(kc[4 + i], kc[2 * i], kc[2 * i + 1], ALU.add, ["KC%d" % (2 * i), "KC%d" % (2 * i + 1)], ["KW%d" % i], 1)
+        if i:
+            tt(kc[5], kc[5], kc[7], ALU.add, ["KW1", "KC7"], ["KW1"], 1)
         ts(T["W%d" % i][:], T.WC[:], kc[4 + i], None, ALU.mult, None, ["WC", "KW%d" % i], ["W%d" % i], 72)
     ts(kc[6], T.KK[:], -LN2, -160.0 * LN2, ALU.mult, ALU.add, ["KK"], ["KE"], 1)
-    for c, x in enumerate((-26.0, 6.0, -10.5, 0.0)):
+    for c, x in enumerate((-26.0, 6.0, -10.5)):
         fill(T.TB[:, c:c + 1], x, ["TB0_%d" % c], 1)
-    TB0 = ["TB0_%d" % c for c in range(4)]
+    TB0 = ["TB0_%d" % c for c in range(3)]
     for c in DIAG:
         ts(dg(c), T.I1[:], c, None, ALU.mult, None, ["I1"], dk(c), 64)
     ts(T.BOH[:], T.B2[:, 0:128], 0.5, None, ALU.mult, None, ["B2"], ["BOH"], 64)
@@ -155,8 +161,8 @@ def build(g, core, T, topo):
         last = t == NV - 1
         st = {}
 
-        def env(b):
-            cur[0] = b
+        def env(b, stage):
+            cur[0], cur[1] = b, stage
             return (lambda n: col(n, b, LB), lambda n: col(n, b, 2 * LB), lambda n: col(n, b, 16 * LB), lambda n: "%s_%d" % (n, b),
                     T["pb%d" % b], "ps%d" % b, T["pb%d" % (4 + b)], "ps%d" % (4 + b))
 
@@ -164,7 +170,7 @@ def build(g, core, T, topo):
             return T[buf][:, 16 * LB * b + k:16 * LB * (b + 1):16]
 
         def begin(b):
-            f1, f2, f16, K, X, kX, Cb, kC = env(b)
+            f1, f2, f16, K, X, kX, Cb, kC = env(b, 0)
             if t == 0:
                 S_, G_, SG_, kS, kG = f1("SI"), f1("GI"), None, "SI", "GI"
                 xf, kx, n = f1("ZN"), "ZN0", 1
@@ -187,7 +193,7 @@ def build(g, core, T, topo):
             act(f1("PB"), f1("PM"), AF.Relu, [K("PM")], [K("PB")], scale=8192.0)
             ga, gb = col("G2", 2 * b, LB), col("G2", 2 * b + 1, LB)
             tt(ga, G_, f1("PB"), ALU.max, [kG, K("PB")], [K("G2a")], 2 * LB)
-            act(gb, ga, AF.Copy, [K("G2a")], [K("G2b")])
+            act(gb, ga, AF.Copy, [K("G2a")], [K("G2b")], bias=32768.0)
             st[b] = (S_, G_, SG_, kS, kG, xf, kx)
 
         for b in range(NB):
@@ -201,12 +207,12 @@ def build(g, core, T, topo):
             cp(c1, pt, [kb], ["PARC%d" % t], 1)
             ts(c2, c1, 1, None, ALU.bitwise_and, None, ["PARC%d" % t], ["PARB%d" % t], 1)
             cp(c3, c2, ["PARB%d" % t], ["PARF%d" % t], 1)
-            ts(T.TB[:, 4 * t:4 * t + 4], T.TB[:, 0:4], c3, None, ALU.subtract, None, TB0 + ["PARF%d" % t], ["TB%d" % t], 4)
+            ts(T.TB[:, 4 * t:4 * t + 3], T.TB[:, 0:3], c3, None, ALU.subtract, None, TB0 + ["PARF%d" % t], ["TB%d" % t], 4)
             TBk = ["TB%d" % t]
         bU, bC, bM = (T.TB[:, 4 * t + j:4 * t + j + 1] for j in range(3))
 
         def step(b, i):
-            f1, f2, f16, K, X, kX, Cb, kC = env(b)
+            f1, f2, f16, K, X, kX, Cb, kC = env(b, (1, 3, 4, 5)[i])
             S_, G_, SG_, kS, kG, xf, kx = st[b]
             lst, kl = (col("LST", 2 * b, LB), K("LS")) if i == 0 else (f1("LA"), K("LA"))
             a, ka = (S_, kS) if i == 0 else (f1("AI"), K("AI")) if t == 0 else (f1("AA"), K("AA"))
@@ -219,12 +225,11 @@ def build(g, core, T, topo):
             mm([(X[:, j * LB:j * LB + LB], w[:, 15 - k:143 - k], strided("PG", b, k), k == 0, k == 15) for j, w in enumerate((T.W0, T.W1)) for k in range(16)],
                32 * LB, ["W0", "W1", K("PG")], [kX])
             tt(f2("FF"), f2("G2"), R_, ALU.is_equal, [K("G2a"), K("G2b"), kX], [K("FF")], 2 * LB)
-            act(f2("XS"), R_, AF.Copy, [kX], [K("XS")], 2 * LB, bias=4096.0 * (i + 1))
+            act(f2("XS"), R_, AF.Copy, [kX], [K("XS")], 2 * LB, bias=4096.0 * (i + 1) - 32768.0)
             tt(f1("MM"), f1("T8"), C_, ALU.is_le, [K("T8"), kC], [K("MM")])
             act(f1("UU"), C_, AF.Relu, [kC] + TBk, [K("UU")], bias=bU)
             P = -32768.0
-            mm([(X_, T.IF[:], f2("XS"), True, False), (X0, dg(P), T.ONE[:, 0:LB], False, False), (X_, dg(P), f2("FF"), False, False)],
-               11 * LB, dk(P) + ["IF", "ONE", K("XS"), K("FF")], [kX])
+            mm([(X_, T.IF[:], f2("XS"), True, False), (X_, dg(P), f2("FF"), False, False)], 10 * LB, dk(P) + ["IF", K("XS"), K("FF")], [kX])
             mm([(X0, dg(-P), f1("MM"), False, False), (X1, dg(P), f1("MM"), False, False)], 2 * LB, dk(P, -P) + [K("MM")], [kX])
             mm([(X0, dg(P), f1("UU"), False, False), (X1, dg(P), f1("UU"), False, True)], 2 * LB, dk(P) + [K("UU")], [kX])
             tt(f1("T1"), a, X0, ALU.max, [ka, kX], [K("T1")])
@@ -238,9 +243,9 @@ def build(g, core, T, topo):
                 cp(f1("LA"), f1("AA"), [K("AA")], [K("LA")])
 
         def covg(b):
-            f1, f2, f16, K, X, kX, Cb, kC = env(b)
+            f1, f2, f16, K, X, kX, Cb, kC = env(b, 2)
             lst, cg, ms = col("LST", 2 * b + 1, LB), Cb[:, LB:2 * LB], Cb[:, 2 * LB:3 * LB]
-            tt(f16("GEG"), T.EV[:, 0:W].indirect(lst), f16("EX"), ALU.is_ge, EVk(1) + [K("LG"), K("EX")], [K("GEG")], 16 * LB * C_GATH, "covg")
+            tt(f16("GEG"), T.EV[:, 0:W].indirect(lst), f16("EX"), ALU.is_ge, EVk(1) + [K("LG"), K("EX")], [K("GEG")], 16 * LB * C_GATH)
             mm([(cg, T.WC[:, 15 - k:143 - k], strided("GEG", b, k), k == 0, k == 15) for k in range(16)], 16 * LB, ["WC", K("GEG")], [kC])
             act(f1("MS"), cg, AF.Sign, [kC] + TBk, [K("MS")], bias=bM)
             mm([(ms, T.BON[:], f1("MS"), True, False), (ms, dg(32.0), f1("PM"), False, True)], 2 * LB, ["BON", K("MS"), K("PM")] + dk(32.0), [kC])
@@ -248,7 +253,7 @@ def build(g, core, T, topo):
             act(f1("UPD"), ms, AF.Relu, [kC], [K("UPD")], bias=-28.0)
 
         def finish(b):
-            f1, f2, f16, K, X, kX, Cb, kC = env(b)
+            f1, f2, f16, K, X, kX, Cb, kC = env(b, 6)
             S_, G_, SG_, kS, kG, xf, kx = st[b]
             C_, cw, sx, nr = Cb[:, 0:LB], Cb[:, 4 * LB:5 * LB], Cb[:, 3 * LB:4 * LB], Cb[:, 6 * LB:7 * LB]
             p4, p5, p45 = X[:, 4 * LB:5 * LB], X[:, 5 * LB:6 * LB], X[:, 4 * LB:6 * LB]
@@ -339,26 +344,23 @@ def link(ops):
         o["dep"] = dep
 
 
-def schedule(ops, par=None):
-    par = par or PAR
-    wake = 0.08
+def schedule(ops, par):
     n = len(ops)
     succ = [[] for _ in range(n)]
     for o in ops:
-        for p in o["dep"]:
-            succ[p].append(o["i"])
+        for p, w in o["dep"].items():
+            succ[p].append((o["i"], w))
     prio = [0.0] * n
-    x = int(par[7])
     for o in reversed(ops):
         m = 0.0
-        for j in succ[o["i"]]:
-            m = max(m, prio[j] + (wake if ops[j]["q"] != o["q"] else 0.0))
+        for j, w in succ[o["i"]]:
+            m = max(m, prio[j] + (WAKE if w else 0.0))
         prio[o["i"]] = m + o["dur"] + o["lat"]
     for o in ops:
-        x = (x * 1103515245 + 12345) % 2147483648
-        prio[o["i"]] += par[o["b"]] - (par[5] if o["name"] == "covg" else 0.0) + par[6] * (x / 2147483648.0 - 0.5)
+        prio[o["i"]] += par[0][o["b"]] + par[2][o["b"]][o["st"]]
     left = [len(o["dep"]) for o in ops]
     rdy = [0.0] * n
+    t0s = [0.0] * n
     free = {}
     avail = {i for i in range(n) if left[i] == 0}
     while avail:
@@ -366,43 +368,85 @@ def schedule(ops, par=None):
         for i in avail:
             o = ops[i]
             t0 = rdy[i] if o["q"] == "R" else max(free.get(o["q"], 0.0), rdy[i])
-            key = (t0 + (par[4] if o["dur"] > 1.0 and o["q"] in "VS" else 0.0), -prio[i], i, t0)
+            key = (t0 + (par[1] if o["dur"] > 1.0 and o["q"] in "VS" else 0.0), -prio[i], i, t0)
             if best is None or key < best:
                 best = key
         i, t0 = best[2:]
         avail.discard(i)
         o = ops[i]
-        o["t0"] = t0
+        t0s[i] = t0
         free[o["q"]] = t0 + o["dur"]
-        for j in succ[i]:
-            p = ops[j]
-            if p["q"] != o["q"]:
-                w = t0 + o["dur"] + o["lat"] + wake
-            else:
-                w = t0 + o["dur"] + (o["lat"] if p["dep"][i] else 0.0)
-            rdy[j] = max(rdy[j], w)
+        for j, w in succ[i]:
+            rdy[j] = max(rdy[j], t0 + o["dur"] + (o["lat"] + WAKE if w else 0.0))
             left[j] -= 1
             if left[j] == 0:
                 avail.add(j)
-    return sorted(ops, key=lambda o: (o["t0"], o["i"])), max(o["t0"] + o["dur"] + o["lat"] for o in ops)
+    return sorted(range(n), key=lambda i: (t0s[i], i))
 
 
-def emit(g, T, ops):
+def span(ops, order, wake, gath, lat):
+    n = len(ops)
+    free, end, beg = {}, [0.0] * n, [0.0] * n
+    for i in order:
+        o = ops[i]
+        q = o["q"]
+        t = 0.0 if q == "R" else free.get(q, 0.0)
+        for p, w in o["dep"].items():
+            t = max(t, end[p] + wake if w else beg[p] + 0.02)
+        d = o["dur"] * (gath if o["dur"] > 1.0 and q in "VS" else 1.0)
+        beg[i] = t
+        free[q] = t + d
+        end[i] = t + d + o["lat"] + (lat if q == "R" else 0.0)
+    return max(end)
+
+
+def search(ops):
+    cases = [(0.17, 1.3, 1.0), (0.12, 1.0, 0.0), (0.17, 1.63, 2.0), (0.25, 1.3, 1.0)]
+    x = [1]
+
+    def rnd(n):
+        x[0] = (x[0] * 1103515245 + 12345) % 2147483648
+        return (x[0] >> 8) % n
+    best, par, norm = None, PAR, None
+    for i in range(TRIES):
+        p = [list(par[0]), par[1], [list(r) for r in par[2]]]
+        if i:
+            k = rnd(10)
+            if k < 3:
+                for j in range(3):
+                    p[0][j] += (rnd(101) - 50) * 0.02
+            elif k < 9:
+                for j in range(1 + rnd(3)):
+                    p[2][rnd(4)][rnd(7)] += (rnd(101) - 50) * 0.06
+            else:
+                p[1] = max(0.0, p[1] + (rnd(101) - 50) * 0.003)
+        order = schedule(ops, p)
+        e = [span(ops, order, *c) for c in cases]
+        norm = norm or e
+        r = [a / b for a, b in zip(e, norm)]
+        val = sum(r) / 4 + 0.3 * max(r)
+        if best is None or val < best[0]:
+            best, par = (val, order, e), p
+    return best
+
+
+def emit(g, T, ops, order):
     queues = {"V": g.vector, "S": g.scalar, "P": g.tensor, "G": g, "Y": g.sync}
     cnt = {}
-    for o in ops:
+    for n, i in enumerate(order):
+        o = ops[i]
         s = o["sem"] or QS[o["q"]]
         cnt[s] = cnt.get(s, 0) + o["inc"]
-        o["tick"] = (s, cnt[s])
-    byi = {o["i"]: o for o in ops}
+        o["tick"], o["pos"] = (s, cnt[s]), n
     know = {q: {} for q in queues}
-    for o in ops:
+    for i in order:
+        o = ops[i]
         if o["q"] == "R":
             o["know"] = {o["tick"][0]: o["tick"][1]}
             continue
         base = dict(know[o["q"]])
         e = queues[o["q"]]
-        for p in sorted((byi[p] for p, w in o["dep"].items() if w), key=lambda p: (-p["t0"], p["i"])):
+        for p in sorted((ops[p] for p, w in o["dep"].items() if w), key=lambda p: -p["pos"]):
             s, c = p["tick"]
             if base.get(s, 0) >= c:
                 continue
@@ -425,6 +469,7 @@ def rank_program(g, core, T, topo):
         return
     ops = build(g, core, T, topo)
     link(ops)
-    ops, est = schedule(ops)
-    emit(g, T, ops)
-    return est
+    if "best" not in ORDER:
+        ORDER["best"] = search(ops)
+    emit(g, T, ops, ORDER["best"][1])
+    return ORDER["best"][2]

import math
from concourse.mybir import AluOpType as ALU, ActivationFunctionType as AF

NB = 4
LB = 256 // NB
NV = 4
W = 4096
ND = [16384, 12288, 8192, 4096]
LN2 = math.log(2.0)
LAT = 7.0
CY, C_GATH, C_PE, WAKE = 0.00083, 1.2, 0.00045, 0.25
PAR = [[6.75, 3.44, 1.87, 0.0], 0.3,
       [[0.0, 0.0, 1.1, 0.0, 0.0, 0.0, 0.0], [0.0, 0.0, 0.6, 0.0, 0.0, 0.0, 0.0], [0.0, 0.5, -0.8, 0.0, 0.0, 0.0, 0.0], [0.3, 0.0, 0.2, 0.0, 0.0, 0.0, 1.1]]]
TRIES = 400
ORDER = {}

SCRATCH = {}
for _n, _k, _t in (("EV", 5 * W, 0), ("PW", 4 * W, 0), ("EX", W, 0), ("GE", W, 0), ("GEG", W, 0), ("PG", W, 0),
                   ("SI", 256, 2), ("GI", 256, 2), ("ZI", 1024, 2), ("ZN", 1024, 1), ("PARI", 256, 2), ("PCI", 1024, 2),
                   ("PCB", 1024, 0), ("LST", 512, 3), ("LA", 256, 3), ("XL", 256, 3), ("XF", 256, 1), ("PB", 256, 1),
                   ("G2", 512, 1), ("PM", 256, 0), ("MM", 256, 0), ("UU", 256, 0), ("FF", 512, 0), ("T1", 256, 1),
                   ("AA", 256, 1), ("AM", 256, 2), ("AI", 256, 2), ("IF", 128, 1), ("MS", 256, 0), ("NF", 256, 0),
                   ("UPD", 256, 0), ("C2", 256, 0), ("MV", 256, 0), ("WW", 256, 0), ("WIN", 256, 0), ("SGN", 256, 0),
                   ("SGM", 512, 2), ("CNT", 32, 1), ("PARC", 4, 2), ("PARB", 4, 2), ("PARF", 4, 1), ("TB", 16, 1),
                   ("LAND", 9 * 256, 2), ("PKT", 9 * 256, 2), ("LANDF", 512, 1), ("PKF", 512, 1), ("ONE", 144, 0),
                   ("XS", 512, 1), ("T8", 256, 0), ("CC", 256, 0), ("B1", 144, 0), ("B2", 144, 0), ("WC", 144, 0),
                   ("W0", 144, 0), ("W1", 144, 0), ("I1", 128, 0), ("BOH", 128, 0), ("BON", 128, 0), ("ON32", 128, 1),
                   ("KI", 1, 2), ("KK", 1, 2), ("KC", 8, 1), ("DG", 128 * 6, 0)):
    SCRATCH[_n] = ("sbuf", [128, _k], ("bfloat16", "float32", "int32", "uint16")[_t])
SCRATCH["SGI"] = ("sbuf", [8, 1024], "int32")
SCRATCH["NSG"] = ("sbuf", [8, 1024], "bfloat16")
SCRATCH["E1"] = ("sbuf", [8, 128], "bfloat16")
SCRATCH["EN"] = ("sbuf", [8, 512], "bfloat16")
for _n in range(8):
    SCRATCH["pb%d" % _n] = ("psum", [128, 512], "float32")
DIAG = [16.0, 32.0, 20480.0, 40960.0, -32768.0, 32768.0]
SEMAPHORES = (["qV", "qS", "qP", "qG", "sent"] + ["d%d" % i for i in range(32)]
              + ["arr%d_%d" % (t, b) for t in range(1, 5) for b in range(NB)])
QS = {"V": "qV", "S": "qS", "P": "qP", "G": "qG"}


def build(g, core, T, topo):
    rank = T.rank_of(core)
    nxt, prv = T.cores[(rank + 1) % 4], T.cores[(rank + 3) % 4]
    n_out, n_arr = len(topo.engines(core, nxt)), len(topo.engines(prv, core))
    rid, pid = topo.addr(nxt)[:2]
    msk = topo.mask(core, nxt)
    ops = []
    ndma = [0]
    cur = [0, 0]
    v, s, te = g.vector, g.scalar, g.tensor

    def op(q, dur, fn, rd=(), wr=(), lat=0.0, sem=None, inc=1, name=""):
        ops.append({"q": q, "dur": dur, "lat": lat, "fn": fn, "rd": list(rd), "wr": list(wr), "sem": sem, "inc": inc,
                    "name": name, "i": len(ops), "b": cur[0], "st": cur[1]})

    def dma(q, out, in_, rd, wr, us):
        ndma[0] += 1
        e = g.sync if q == "Y" else s
        op(q, 0.07, lambda: e.dma_start(out, in_), rd, wr, lat=us, sem="d%d" % (ndma[0] - 1), inc=16, name="dma")

    def vec(n, fn, rd, wr):
        op("V", max(64, n) * CY + 0.01, fn, rd, wr)

    def tt(out, a, b, o, rd, wr, n=LB):
        vec(n, lambda: v.tensor_tensor(out, a, b, o), rd, wr)

    def ts(out, a, s1, s2, o0, o1, rd, wr, n=LB):
        vec(n, (lambda: v.tensor_scalar(out, a, s1, s2, o0)) if o1 is None else (lambda: v.tensor_scalar(out, a, s1, s2, o0, o1)), rd, wr)

    def cp(out, a, rd, wr, n=LB):
        vec(n, lambda: v.tensor_copy(out, a), rd, wr)

    def fill(out, x, wr, n):
        vec(n, lambda: v.memset(out, x), [], wr)

    def act(out, a, f, rd, wr, n=LB, **kw):
        op("S", max(64, n) * CY + 0.03, lambda: s.activation(out, a, f, **kw), rd, wr)

    def mm(calls, cols, rd, wr):
        def fn():
            for c in calls:
                x = te.matmul(*c)
            return x
        op("P", cols * C_PE + 0.02, fn, rd, wr)

    def dg(c):
        i = DIAG.index(c)
        return T.DG[:, 128 * i:128 * i + 128]

    def dk(*c):
        return ["DG%g" % x for x in c]

    def col(n, t, w=256):
        return T[n][:, w * t:w * t + w]

    dma("Y", T.EV[:, 0:W], T.ev[:], [], ["EV0"], 6.0)
    dma("S", T.PARI[:], T.par[:], [], ["PARI"], 2.0)
    dma("S", col("ZI", 0), T.z[:, 0:256], [], ["ZI0"], 2.0)
    dma("S", T.SI[:], T.s0[:], [], ["SI"], 2.5)
    dma("S", T.SGI[:], T.sg[:], [], ["SGI"], 2.5)
    dma("S", T.GI[:], T.g0[:], [], ["GI"], 3.0)
    fill(T.ONE[:], 1.0, ["ONE"], 72)
    fill(T.PW[:, 0:W], 1.0, ["PW0m"], 2048)
    fill(T.SGN[:], -1.0, ["SGN"], 64)
    op("G", 0.15, lambda: g.iota(T.KI[:], [[0, 1]], 0, 1), [], ["KI"])

    def sel(out, a, pat, cop, base, cm, rd, wr):
        op("G", 0.4, lambda: g.affine_select(out, a, pat, cop, 0.0, base, cm), [rd], [wr])
    sel(T.B1[:], T.ONE[:], [[-16, 9], [0, 16]], ALU.is_ge, 0, 1, "ONE", "B1")
    sel(T.B2[:], T.B1[:], [[16, 9], [0, 16]], ALU.is_ge, 15, -1, "B1", "B2")
    sel(T.WC[:], T.B2[:], [[0, 9], [1, 16]], ALU.is_equal, -15, 0, "B2", "WC")
    sel(T.I1[:], T.ONE[:, 0:128], [[-1, 128]], ALU.is_equal, 0, 1, "ONE", "I1")
    sel(T.E1[:], T.ONE[0:8, 0:128], [[1, 8], [0, 16]], ALU.is_equal, 0, -1, "ONE", "E1")
    for i in range(4):
        ts(col("PCI", i), T.PARI[:], 6 * i, 63, ALU.logical_shift_right, ALU.bitwise_and, ["PARI"], ["PCI%d" % i], 256)
    for i in range(4):
        cp(col("PCB", i), col("PCI", i), ["PCI%d" % i], ["PCB%d" % i], 256)
        dma("Y", T.PW[i::16, 0:W], col("PCB", i), ["PCB%d" % i, "PW0m"], ["PW0p%d" % i], 2.0)
    PW0 = ["PW0m"] + ["PW0p%d" % i for i in range(4)]
    kc = [T.KC[:, i:i + 1] for i in range(8)]
    ts(T.KK[:], T.KI[:], 15, None, ALU.bitwise_and, None, ["KI"], ["KK"], 1)
    for i in range(4):
        ts(kc[i], T.KK[:], float(i), (1.0, 64.0)[i % 2], ALU.is_equal, ALU.mult, ["KK"], ["KC%d" % i], 1)
    ts(kc[7], T.KK[:], 4.0, 32768.0, ALU.is_equal, ALU.mult, ["KK"], ["KC7"], 1)
    for i in range(2):
        tt(kc[4 + i], kc[2 * i], kc[2 * i + 1], ALU.add, ["KC%d" % (2 * i), "KC%d" % (2 * i + 1)], ["KW%d" % i], 1)
        if i:
            tt(kc[5], kc[5], kc[7], ALU.add, ["KW1", "KC7"], ["KW1"], 1)
        ts(T["W%d" % i][:], T.WC[:], kc[4 + i], None, ALU.mult, None, ["WC", "KW%d" % i], ["W%d" % i], 72)
    ts(kc[6], T.KK[:], -LN2, -160.0 * LN2, ALU.mult, ALU.add, ["KK"], ["KE"], 1)
    for c, x in enumerate((-26.0, 6.0, -10.5)):
        fill(T.TB[:, c:c + 1], x, ["TB0_%d" % c], 1)
    TB0 = ["TB0_%d" % c for c in range(3)]
    for c in DIAG:
        ts(dg(c), T.I1[:], c, None, ALU.mult, None, ["I1"], dk(c), 64)
    ts(T.BOH[:], T.B2[:, 0:128], 0.5, None, ALU.mult, None, ["B2"], ["BOH"], 64)
    ts(T.BON[:], T.B2[:, 0:128], -0.5, None, ALU.mult, None, ["B2"], ["BON"], 64)
    for t in range(NV):
        if t:
            dma("Y", col("ZI", t), T.z[:, 256 * t:256 * t + 256], [], ["ZI%d" % t], 2.0)
        ts(col("NSG", t), col("SGI", t), -1.0, 1.0, ALU.mult, ALU.add, ["SGI"], ["NSG%d" % t], 256)
        ts(col("EN", t, 128), T.E1[:], float(ND[t]), None, ALU.mult, None, ["E1"], ["EN%d" % t], 64)
        bk, pt = "ps%d" % t, T["pb%d" % t][:, 0:256]
        mm([(pt, col("EN", t, 128), col("NSG", t), True, True)], 256, ["EN%d" % t, "NSG%d" % t], [bk])
        tt(col("ZN", t), col("ZI", t), pt, ALU.add, ["ZI%d" % t, bk], ["ZN%d" % t], 256)
    fill(T.ON32[:], 1.0 / 32, ["ON32"], 128)
    cp(T.IF[:], T.I1[:], ["I1"], ["IF"], 128)
    for r in range(1, 4):
        dma("Y", col("EV", r, W), T.ev[:], [], ["EV%d" % r], 6.0)
        dma("Y", col("PW", r, W), T.PW[:, 0:W], PW0, ["PW%d" % r], 6.0)
    dma("Y", col("EV", 4, W), T.ev[:], [], ["EV4"], 6.0)

    def EVk(n):
        return ["EV%d" % r for r in range(n)]

    def PWk(n):
        return PW0 + ["PW%d" % r for r in range(1, n)]

    def visit(t):
        last = t == NV - 1
        st = {}

        def env(b, stage):
            cur[0], cur[1] = b, stage
            return (lambda n: col(n, b, LB), lambda n: col(n, b, 2 * LB), lambda n: col(n, b, 16 * LB), lambda n: "%s_%d" % (n, b),
                    T["pb%d" % b], "ps%d" % b, T["pb%d" % (4 + b)], "ps%d" % (4 + b))

        def strided(buf, b, k):
            return T[buf][:, 16 * LB * b + k:16 * LB * (b + 1):16]

        def begin(b):
            f1, f2, f16, K, X, kX, Cb, kC = env(b, 0)
            if t == 0:
                S_, G_, SG_, kS, kG = f1("SI"), f1("GI"), None, "SI", "GI"
                xf, kx, n = f1("ZN"), "ZN0", 1
                cp(f1("XL"), f1("ZI"), ["ZI0"], [K("XL")])
                cp(col("LST", 2 * b, LB), S_, [kS], [K("LS")])
                cp(col("LST", 2 * b + 1, LB), G_, [kG], [K("LG")])
            else:
                o = ((t - 1) * NB + b) * 3 * LB
                S_, G_, R_, SG_ = (T.LAND[:, o + x * LB:o + y * LB] for x, y in ((0, 1), (1, 2), (2, 3), (0, 2)))
                kS = kG = "LAND%d_%d" % (t, b)
                xf, kx, n = f1("XF"), K("XF"), 5
                tt(xf, col("ZN", NB * t + b, LB), R_, ALU.max, ["ZN%d" % t, kS], [kx], 2 * LB)
                cp(f1("XL"), xf, [kx], [K("XL")])
                cp(f2("LST"), SG_, [kS], [K("LS"), K("LG")], 2 * LB)
            act(f16("EX"), T.EV[:, 0:n * W].indirect(f1("XL")), AF.Copy, EVk(n) + [K("XL")], [K("EX")], 16 * LB * C_GATH)
            act(f1("PM"), xf, AF.Sign, [kx], [K("PM")], bias=4095.5, scale=-1.0)
            if t:
                act(f1("MV"), xf, AF.Sign, [kx], [K("MV"), "CNT%d_%d" % (t, b)], bias=-(ND[t - 1] - 0.5), accum_out=T.CNT[:, 8 * t + b:8 * t + b + 1])
            act(f1("T8"), f1("PM"), AF.Copy, [K("PM")], [K("T8")], scale=16.0, bias=8.0)
            act(f1("PB"), f1("PM"), AF.Relu, [K("PM")], [K("PB")], scale=8192.0)
            ga, gb = col("G2", 2 * b, LB), col("G2", 2 * b + 1, LB)
            tt(ga, G_, f1("PB"), ALU.max, [kG, K("PB")], [K("G2a")], 2 * LB)
            act(gb, ga, AF.Copy, [K("G2a")], [K("G2b")], bias=32768.0)
            st[b] = (S_, G_, SG_, kS, kG, xf, kx)

        for b in range(NB):
            begin(b)
        TBk = TB0
        if t:
            pt, kb = T["pb%d" % (3 + NB)][:, 448:449], "ps%d" % (3 + NB)
            c1, c2, c3 = (T[n][:, t:t + 1] for n in ("PARC", "PARB", "PARF"))
            mm([(pt, T.ON32[:], T.CNT[:, 8 * t + j:8 * t + j + 1], j == 0, j == NB - 1) for j in range(NB)], 4 * 256,
               ["ON32"] + ["CNT%d_%d" % (t, j) for j in range(NB)], [kb])
            cp(c1, pt, [kb], ["PARC%d" % t], 1)
            ts(c2, c1, 1, None, ALU.bitwise_and, None, ["PARC%d" % t], ["PARB%d" % t], 1)
            cp(c3, c2, ["PARB%d" % t], ["PARF%d" % t], 1)
            ts(T.TB[:, 4 * t:4 * t + 3], T.TB[:, 0:3], c3, None, ALU.subtract, None, TB0 + ["PARF%d" % t], ["TB%d" % t], 4)
            TBk = ["TB%d" % t]
        bU, bC, bM = (T.TB[:, 4 * t + j:4 * t + j + 1] for j in range(3))

        def step(b, i):
            f1, f2, f16, K, X, kX, Cb, kC = env(b, (1, 3, 4, 5)[i])
            S_, G_, SG_, kS, kG, xf, kx = st[b]
            lst, kl = (col("LST", 2 * b, LB), K("LS")) if i == 0 else (f1("LA"), K("LA"))
            a, ka = (S_, kS) if i == 0 else (f1("AI"), K("AI")) if t == 0 else (f1("AA"), K("AA"))
            n = 1 if t == 0 else i + 1
            C_, R_, X0, X1, X_ = Cb[:, 0:LB], X[:, 0:2 * LB], X[:, 2 * LB:3 * LB], X[:, 3 * LB:4 * LB], X[:, 2 * LB:4 * LB]
            tt(f16("GE"), T.EV[:, 0:n * W].indirect(lst), f16("EX"), ALU.is_ge, EVk(n) + [kl, K("EX")], [K("GE")], 16 * LB * C_GATH)
            act(f16("PG"), T.PW[:, 0:n * W].indirect(lst), AF.Copy, PWk(n) + [kl], [K("PG")], 16 * LB * C_GATH)
            mm([(C_, dg(16.0), f1("PM"), True, False)] + [(C_, T.WC[:, 15 - k:143 - k], strided("GE", b, k), False, k == 15) for k in range(16)],
               17 * LB, ["WC", K("GE"), K("PM")] + dk(16.0), [kC])
            mm([(X[:, j * LB:j * LB + LB], w[:, 15 - k:143 - k], strided("PG", b, k), k == 0, k == 15) for j, w in enumerate((T.W0, T.W1)) for k in range(16)],
               32 * LB, ["W0", "W1", K("PG")], [kX])
            tt(f2("FF"), f2("G2"), R_, ALU.is_equal, [K("G2a"), K("G2b"), kX], [K("FF")], 2 * LB)
            act(f2("XS"), R_, AF.Copy, [kX], [K("XS")], 2 * LB, bias=4096.0 * (i + 1) - 32768.0)
            tt(f1("MM"), f1("T8"), C_, ALU.is_le, [K("T8"), kC], [K("MM")])
            act(f1("UU"), C_, AF.Relu, [kC] + TBk, [K("UU")], bias=bU)
            P = -32768.0
            mm([(X_, T.IF[:], f2("XS"), True, False), (X_, dg(P), f2("FF"), False, False)], 10 * LB, dk(P) + ["IF", K("XS"), K("FF")], [kX])
            mm([(X0, dg(-P), f1("MM"), False, False), (X1, dg(P), f1("MM"), False, False)], 2 * LB, dk(P, -P) + [K("MM")], [kX])
            mm([(X0, dg(P), f1("UU"), False, False), (X1, dg(P), f1("UU"), False, True)], 2 * LB, dk(P) + [K("UU")], [kX])
            tt(f1("T1"), a, X0, ALU.max, [ka, kX], [K("T1")])
            if t == 0 and i < 3:
                tt(f1("AM"), f1("T1"), X1, ALU.max, [K("T1"), kX], [K("AM")])
                ts(f1("AI"), f1("AM"), 4095, None, ALU.bitwise_and, None, [K("AM")], [K("AI")])
                cp(f1("LA"), f1("AI"), [K("AI")], [K("LA")])
                return
            tt(f1("AA"), f1("T1"), X1, ALU.max, [K("T1"), kX], [K("AA")])
            if i < 3:
                cp(f1("LA"), f1("AA"), [K("AA")], [K("LA")])

        def covg(b):
            f1, f2, f16, K, X, kX, Cb, kC = env(b, 2)
            lst, cg, ms = col("LST", 2 * b + 1, LB), Cb[:, LB:2 * LB], Cb[:, 2 * LB:3 * LB]
            tt(f16("GEG"), T.EV[:, 0:W].indirect(lst), f16("EX"), ALU.is_ge, EVk(1) + [K("LG"), K("EX")], [K("GEG")], 16 * LB * C_GATH)
            mm([(cg, T.WC[:, 15 - k:143 - k], strided("GEG", b, k), k == 0, k == 15) for k in range(16)], 16 * LB, ["WC", K("GEG")], [kC])
            act(f1("MS"), cg, AF.Sign, [kC] + TBk, [K("MS")], bias=bM)
            mm([(ms, T.BON[:], f1("MS"), True, False), (ms, dg(32.0), f1("PM"), False, True)], 2 * LB, ["BON", K("MS"), K("PM")] + dk(32.0), [kC])
            act(f1("NF"), ms, AF.Relu, [kC], [K("NF")], bias=40.0)
            act(f1("UPD"), ms, AF.Relu, [kC], [K("UPD")], bias=-28.0)

        def finish(b):
            f1, f2, f16, K, X, kX, Cb, kC = env(b, 6)
            S_, G_, SG_, kS, kG, xf, kx = st[b]
            C_, cw, sx, nr = Cb[:, 0:LB], Cb[:, 4 * LB:5 * LB], Cb[:, 3 * LB:4 * LB], Cb[:, 6 * LB:7 * LB]
            p4, p5, p45 = X[:, 4 * LB:5 * LB], X[:, 5 * LB:6 * LB], X[:, 4 * LB:6 * LB]
            act(f1("CC"), C_, AF.Copy, [kC], [K("CC")])
            act(f1("C2"), C_, AF.Relu, [kC] + TBk, [K("C2")], bias=bC)
            mm([(cw, T.I1[:], f1("CC"), True, False)] + [(cw, dg(32.0), f1(n), False, False) for n in ("NF", "C2")], 3 * LB,
               dk(32.0) + ["I1", K("CC"), K("NF"), K("C2")], [kC])
            act(f1("MV"), f1("AA"), AF.Relu, [K("AA")], [K("MV")], bias=-16383.0)
            mm([(cw, dg(32.0), f1("MV"), False, True)], LB, dk(32.0) + [K("MV")], [kC])
            act(f1("WW"), cw, AF.Exp, [kC, "KE"], [K("WW")], bias=kc[6], scale=-16.0 * LN2)
            mm([(sx, T.BOH[:], f1("WW"), True, False), (sx, T.I1[:], f1("NF"), False, True)], 2 * LB, ["BOH", "I1", K("WW"), K("NF")], [kC])
            tt(f1("WIN"), f1("WW"), sx, ALU.is_gt, [K("WW"), kC], [K("WIN")])
            o = (t * NB + b) * 3 * LB
            kp, ka, kb = "PKT%d_%d" % (t, b), K("SGMa"), K("SGMb")
            if not last:
                ts(nr, sx, 0.0, -65536.0, ALU.is_gt, ALU.mult, [kC], [kC])
                tt(T.PKT[:, o + 2 * LB:o + 3 * LB], xf, nr, ALU.add, [kx, kC], [kp + "R"])
            c1, c2 = 20480.0, 40960.0
            mm([(p4, dg(c1), f1("PM"), True, False), (p4, T.IF[:], f1("AA"), False, True), (p5, dg(c1), f1("SGN"), True, False),
                (p5, T.IF[:], f1("AA"), False, False), (p5, dg(c2), f1("UPD"), False, False)], 11 * LB,
               dk(c1, c2) + ["IF", "SGN", K("PM"), K("UPD"), K("AA")], [kX])
            mm([(p5, dg(c2), f1("WIN"), False, True)], LB, dk(c2) + [K("WIN")], [kX])
            if t == 0:
                tt(col("SGM", 2 * b, LB), S_, p4, ALU.max, [kS, kX], [ka])
                tt(col("SGM", 2 * b + 1, LB), G_, p5, ALU.max, [kG, kX], [kb])
            else:
                tt(f2("SGM"), SG_, p45, ALU.max, [kS, kX], [ka, kb], 2 * LB)
            out, src = (T.LANDF, T.PKF) if last else (T.LAND, T.PKT)
            w, o = (2 * LB, 2 * LB * b) if last else (3 * LB, o)
            if not last:
                ts(T.PKT[:, o:o + 2 * LB], f2("SGM"), 4095, None, ALU.bitwise_and, None, [ka, kb], [kp + "S"], 2 * LB)
            else:
                ts(f2("SGM"), f2("SGM"), 4095, None, ALU.bitwise_and, None, [ka, kb], [ka, kb], 2 * LB)
                cp(f2("PKF"), f2("SGM"), [ka, kb], [kp + "S"], 2 * LB)
            sem, kl = "arr%d_%d" % (t + 1, b), "LAND%d_%d" % (t + 1, b)
            op("G", 1.0, lambda: g.remote_dma(out[:, o:o + w], src[:, o:o + w], T.sem[sem], T.sem.sent, pid, rid, msk),
               [kp + "S"] + ([] if last else [kp + "R"]), [kp + "sent"], sem="sent", inc=n_out, name="send")
            op("R", 0.0, None, [kp + "sent"], [kl], lat=LAT - 1.0, sem=sem, inc=n_arr, name="arrive")
            if last:
                dma("Y", T.ys[:, LB * b:LB * b + LB], T.LANDF[:, o:o + LB], [kl], ["YS%d" % b], 2.0)
                dma("S", T.yg[:, LB * b:LB * b + LB], T.LANDF[:, o + LB:o + 2 * LB], [kl], ["YG%d" % b], 2.0)

        for b in range(NB):
            step(b, 0)
        for b in range(NB):
            covg(b)
        for i in range(1, 4):
            for b in range(NB):
                step(b, i)
        for b in range(NB):
            finish(b)

    for t in range(NV):
        visit(t)
    return ops


def link(ops):
    lastw, readers, acc = {}, {}, {}
    for o in ops:
        dep = {}

        def add(p, w):
            if p is not o:
                dep[p["i"]] = dep.get(p["i"], False) or w
        for k in o["rd"] + o["wr"]:
            if k[:2] == "ps":
                for q, p in acc.get(k, {}).items():
                    add(p, not (q == o["q"] and q in ("P", "S")))
        for k in o["rd"]:
            if k in lastw:
                p = lastw[k]
                add(p, not (k[:2] == "ps" and p["q"] == "P" and o["q"] == "P"))
        for k in o["wr"]:
            if k[:2] != "ps":
                if k in lastw:
                    add(lastw[k], True)
                for p in readers.get(k, []):
                    add(p, p["q"] != o["q"] or p["sem"] is not None)
        for k in o["rd"]:
            readers.setdefault(k, []).append(o)
        for k in o["wr"]:
            lastw[k] = o
            readers[k] = []
        for k in o["rd"] + o["wr"]:
            if k[:2] == "ps":
                acc.setdefault(k, {})[o["q"]] = o
        o["dep"] = dep


def schedule(ops, par):
    n = len(ops)
    succ = [[] for _ in range(n)]
    for o in ops:
        for p, w in o["dep"].items():
            succ[p].append((o["i"], w))
    prio = [0.0] * n
    for o in reversed(ops):
        m = 0.0
        for j, w in succ[o["i"]]:
            m = max(m, prio[j] + (WAKE if w else 0.0))
        prio[o["i"]] = m + o["dur"] + o["lat"]
    for o in ops:
        prio[o["i"]] += par[0][o["b"]] + par[2][o["b"]][o["st"]]
    left = [len(o["dep"]) for o in ops]
    rdy = [0.0] * n
    t0s = [0.0] * n
    free = {}
    avail = {i for i in range(n) if left[i] == 0}
    while avail:
        best = None
        for i in avail:
            o = ops[i]
            t0 = rdy[i] if o["q"] == "R" else max(free.get(o["q"], 0.0), rdy[i])
            key = (t0 + (par[1] if o["dur"] > 1.0 and o["q"] in "VS" else 0.0), -prio[i], i, t0)
            if best is None or key < best:
                best = key
        i, t0 = best[2:]
        avail.discard(i)
        o = ops[i]
        t0s[i] = t0
        free[o["q"]] = t0 + o["dur"]
        for j, w in succ[i]:
            rdy[j] = max(rdy[j], t0 + o["dur"] + (o["lat"] + WAKE if w else 0.0))
            left[j] -= 1
            if left[j] == 0:
                avail.add(j)
    return sorted(range(n), key=lambda i: (t0s[i], i))


def span(ops, order, wake, gath, lat):
    n = len(ops)
    free, end, beg = {}, [0.0] * n, [0.0] * n
    for i in order:
        o = ops[i]
        q = o["q"]
        t = 0.0 if q == "R" else free.get(q, 0.0)
        for p, w in o["dep"].items():
            t = max(t, end[p] + wake if w else beg[p] + 0.02)
        d = o["dur"] * (gath if o["dur"] > 1.0 and q in "VS" else 1.0)
        beg[i] = t
        free[q] = t + d
        end[i] = t + d + o["lat"] + (lat if q == "R" else 0.0)
    return max(end)


def search(ops):
    cases = [(0.17, 1.3, 1.0), (0.12, 1.0, 0.0), (0.17, 1.63, 2.0), (0.25, 1.3, 1.0)]
    x = [1]

    def rnd(n):
        x[0] = (x[0] * 1103515245 + 12345) % 2147483648
        return (x[0] >> 8) % n
    best, par, norm = None, PAR, None
    for i in range(TRIES):
        p = [list(par[0]), par[1], [list(r) for r in par[2]]]
        if i:
            k = rnd(10)
            if k < 3:
                for j in range(3):
                    p[0][j] += (rnd(101) - 50) * 0.02
            elif k < 9:
                for j in range(1 + rnd(3)):
                    p[2][rnd(4)][rnd(7)] += (rnd(101) - 50) * 0.06
            else:
                p[1] = max(0.0, p[1] + (rnd(101) - 50) * 0.003)
        order = schedule(ops, p)
        e = [span(ops, order, *c) for c in cases]
        norm = norm or e
        r = [a / b for a, b in zip(e, norm)]
        val = sum(r) / 4 + 0.3 * max(r)
        if best is None or val < best[0]:
            best, par = (val, order, e), p
    return best


def emit(g, T, ops, order):
    queues = {"V": g.vector, "S": g.scalar, "P": g.tensor, "G": g, "Y": g.sync}
    cnt = {}
    for n, i in enumerate(order):
        o = ops[i]
        s = o["sem"] or QS[o["q"]]
        cnt[s] = cnt.get(s, 0) + o["inc"]
        o["tick"], o["pos"] = (s, cnt[s]), n
    know = {q: {} for q in queues}
    for i in order:
        o = ops[i]
        if o["q"] == "R":
            o["know"] = {o["tick"][0]: o["tick"][1]}
            continue
        base = dict(know[o["q"]])
        e = queues[o["q"]]
        for p in sorted((ops[p] for p, w in o["dep"].items() if w), key=lambda p: -p["pos"]):
            s, c = p["tick"]
            if base.get(s, 0) >= c:
                continue
            e.wait_ge(T.sem[s], c)
            for s2, c2 in p["know"].items():
                base[s2] = max(base.get(s2, 0), c2)
            base[s] = max(base.get(s, 0), c)
        know[o["q"]] = base
        x = o["fn"]()
        if o["name"] != "send":
            x.then_inc(T.sem[o["tick"][0]], o["inc"])
        o["know"] = dict(base)
        o["know"][o["tick"][0]] = o["tick"][1]
    for s, c in cnt.items():
        g.wait_ge(T.sem[s], c)


def rank_program(g, core, T, topo):
    if T.rank_of(core) is None:
        return
    ops = build(g, core, T, topo)
    link(ops)
    if "best" not in ORDER:
        ORDER["best"] = search(ops)
    emit(g, T, ops, ORDER["best"][1])
    return ORDER["best"][2]
